import numpy as np
import ml_dtypes


def mxq(x, axis, fmt="e4m3"):
    dtype, down = {"e4m3": (ml_dtypes.float8_e4m3fn, 7), "e5m2": (ml_dtypes.float8_e5m2, 14)}[fmt]
    v = np.moveaxis(np.asarray(x, np.float32).astype(ml_dtypes.bfloat16).astype(np.float64), axis, -1)
    blocks = v.reshape(v.shape[:-1] + (-1, 32))
    amax = np.abs(blocks).max(-1, keepdims=True)
    byte = np.maximum(np.where(amax > 0, np.frexp(amax)[1] - 1 + 127, 0) - down, 1)
    scale = np.exp2(byte - 127.0)
    codes = (blocks / scale).astype(np.float32).astype(dtype).astype(np.float64)
    return np.moveaxis((codes * scale).reshape(v.shape), -1, axis)


WIDE = False


def mx_kscale(k):
    if not WIDE:
        return np.ones(k)
    levels = np.array([10, -10, 5, -5, 0])
    if k % 512:
        return np.exp2(np.random.permutation(np.resize(levels, k // 32))).repeat(32)
    a = np.empty((k // 512, 16))
    for p in range(k // 512):
        a[p, :8] = np.random.permutation(np.resize(levels, 8))
        for g in range(8):
            far = levels[np.abs(levels - a[p, g]) >= 10]
            a[p, g + 8] = far[np.random.randint(len(far))]
    return np.exp2(a.ravel()).repeat(32)


def f64(x):
    return np.asarray(x).astype(np.float64)


def striped(idx):
    return np.tile(idx.reshape(-1, 16).T, (8, 1)).astype(np.uint16)


def unstriped(offs):
    return offs[:16].T.reshape(-1).astype(np.int64)


def striped8(idx):
    return np.concatenate([x.reshape(-1, 16).T for x in idx]).astype(np.uint16)


def runs(offs, k):
    lists = np.stack([offs[16 * r : 16 * r + 16].T.reshape(-1) for r in range(8)]).astype(np.int64)
    return lists[np.arange(k) % 512 // 64]


def pack_weight(w):
    k, n = w.shape
    w = f64(np.asarray(w, np.float32).astype(ml_dtypes.bfloat16)).reshape(k // 32, 32, n)
    amax = np.abs(w).max(1)
    byte = np.clip(np.where(amax > 0, np.frexp(amax)[1] - 1 + 127 - 7, 1), 1, 254)
    scaled = (w * np.exp2(127.0 - byte)[:, None, :]).reshape(k, n).astype(np.float32)
    words = np.ascontiguousarray(scaled.reshape(k // 512, 128, 4, n).transpose(0, 1, 3, 2)).astype(ml_dtypes.float8_e4m3fn).view(np.uint8)
    return words, np.ascontiguousarray(byte.astype(np.uint8).reshape(k // 512, 16, n))


def unpack_weight(words, scales):
    g, p, n, _ = words.shape
    vals = np.ascontiguousarray(words).view(ml_dtypes.float8_e4m3fn).astype(np.float64) * np.repeat(np.exp2(scales.astype(np.float64) - 127.0), 8, axis=1)[..., None]
    return vals.transpose(0, 1, 3, 2).reshape(g * 512, n)


E2M1 = np.array([0.0, 0.5, 1.0, 1.5, 2.0, 3.0, 4.0, 6.0, -0.0, -0.5, -1.0, -1.5, -2.0, -3.0, -4.0, -6.0])


def pack_fp4(w):
    k, n = w.shape
    w = f64(np.asarray(w, np.float32).astype(ml_dtypes.bfloat16)).reshape(k // 32, 32, n)
    amax = np.abs(w).max(1)
    mant, ex = np.frexp(amax / 6.0)
    byte = np.clip(np.where(amax > 0, np.where(mant > 0.5, ex, ex - 1) + 127, 1), 1, 254)
    scaled = (w * np.exp2(127.0 - byte)[:, None, :]).reshape(k, n).astype(np.float32)
    c = np.ascontiguousarray(scaled.reshape(k // 512, 128, 4, n).transpose(0, 1, 3, 2)).astype(ml_dtypes.float4_e2m1fn).view(np.uint8) & 0xF
    words = (c[..., 0::2] | (c[..., 1::2] << 4)).reshape(k // 512, 128, 2 * n)
    return np.ascontiguousarray(words), np.ascontiguousarray(byte.astype(np.uint8).reshape(k // 512, 16, n))


def unpack_fp4(words, scales):
    g, _, n = scales.shape
    words = np.ascontiguousarray(words).reshape(g, 128, n, 2)
    nib = np.empty((g, 128, n, 4), np.uint8)
    nib[..., 0::2] = words & 0xF
    nib[..., 1::2] = words >> 4
    vals = E2M1[nib] * np.repeat(np.exp2(scales.astype(np.float64) - 127.0), 8, axis=1)[..., None]
    return vals.transpose(0, 1, 3, 2).reshape(g * 512, n)


K, T, S, N, G, H, W, U = 512, 1024, 256, 512, 2048, 512, 128, 1024


def setup_inputs():
    n = np.random.standard_normal
    s = mx_kscale(K)[:, None]
    u = mx_kscale(K)
    packed_xT = pack_weight(n((K, T)) * s)
    packed_dT = pack_weight(n((K, G)) / s)
    packed_w1 = pack_fp4(n((H, N)) / np.sqrt(H) / u[:, None])
    perm = np.random.permutation(S)
    return {
        "x_words": packed_xT[0],
        "x_scales": packed_xT[1],
        "d_words": packed_dT[0],
        "d_scales": packed_dT[1],
        "gn": (np.random.uniform(0.5, 1.5, (H, 1)) * u[:, None]).astype(np.float32),
        "w1_words": packed_w1[0],
        "w1_scales": packed_w1[1],
        "offs": striped8(np.random.randint(0, T, (8, S))),
        "ka": striped8(np.random.randint(0, G, (8, H))),
        "kb": striped8(np.random.randint(0, G, (8, H))),
        "n1": striped(perm[:W]),
        "n2": striped(perm[W:]),
        "n3": striped(np.random.permutation(S)),
        "n4": striped(np.random.permutation(U)[:S]),
        "n5": striped(np.random.permutation(S)),
    }


def reference(x_words, x_scales, d_words, d_scales, gn, w1_words, w1_scales, offs, ka, kb, n1, n2, n3, n4, n5):
    d_ka = unpack_weight(d_words, d_scales)[np.arange(K)[:, None], runs(ka, K)]
    xq = unpack_weight(x_words, x_scales)[np.arange(K)[:, None], runs(offs, K)]
    d_kb = unpack_weight(d_words, d_scales)[np.arange(K)[:, None], runs(kb, K)]
    h = 0.0625 * (d_ka.T @ xq + d_kb.T @ xq)
    pa = h[:, unstriped(n1)]
    pb = h[:, unstriped(n2)]
    rb = np.minimum(pa, pb)
    ra = np.maximum(pa, pb)
    ds = np.zeros((H, S))
    ds[:, unstriped(n1)] = ra
    dt = ds.copy()
    dt[:, unstriped(n2)] = rb
    z = f64(gn) * (dt - dt[:, unstriped(n3)])
    h2 = unpack_fp4(w1_words, w1_scales).T @ mxq(z, 0, "e4m3")
    nw = np.maximum(h2, h2[:, unstriped(n5)])
    out = np.zeros((N, U))
    out[:, unstriped(n4)] = nw
    return out

@@ -1,0 +1,217 @@
+from contextlib import ExitStack
+
+import concourse.mybir as mybir
+
+K, T, S, N, G, H, W, U = 512, 1024, 256, 512, 2048, 512, 128, 1024
+FLOPS = 2 * (2 * K * H * S + H * N * S)
+
+F32 = mybir.dt.float32
+BF16 = mybir.dt.bfloat16
+I32 = mybir.dt.int32
+U32 = mybir.dt.uint32
+U16 = mybir.dt.uint16
+U8 = mybir.dt.uint8
+FP8X4 = mybir.dt.float8_e4m3fn_x4
+FP4X4 = mybir.dt.float4_e2m1fn_x4
+ALU = mybir.AluOpType
+COPY = mybir.ActivationFunctionType.Copy
+
+P = 128
+PACK = 4
+HALF = S // 2
+
+
+def tile_picked_haqorddpags_none_p_kernel(
+    tc, x_words, x_scales, d_words, d_scales, gn, w1_words, w1_scales, offs, ka, kb, n1, n2, n3, n4, n5, out
+):
+    nc = tc.nc
+    with ExitStack() as ctx:
+        keep = ctx.enter_context(tc.tile_pool(name="keep", bufs=1))
+        psum = ctx.enter_context(tc.psum_pool(name="psum", bufs=1))
+
+        def load_list(name, src):
+            tile = keep.tile(list(src.shape), U16, name=name)
+            nc.sync.dma_start(tile[:], src)
+            return tile
+
+        x_bytes = keep.tile([P, T], U8, name="x_bytes")
+        d_bytes = keep.tile([P, G], U8, name="d_bytes")
+        for tile, rows in ((d_bytes, d_scales), (x_bytes, x_scales)):
+            words = rows[0].bitcast(I32)
+            nc.sync.dma_start(tile[:].bitcast(I32), words.unsqueeze(1).broadcast_to([16, 8, words.shape[1]]))
+
+        ka_l = load_list("ka_l", ka)
+        kb_l = load_list("kb_l", kb)
+        offs_l = load_list("offs_l", offs)
+        d_tab = keep.tile([P, G], U32, name="d_tab", tag="d_then_page")
+        x_tab = keep.tile([P, T], U32, name="x_tab", tag="x_then_page")
+        nc.sync.dma_start(d_tab[:].bitcast(I32), d_words[0].rearrange("p n t -> p (n t)").bitcast(I32))
+        nc.sync.dma_start(x_tab[:].bitcast(I32), x_words[0].rearrange("p n t -> p (n t)").bitcast(I32))
+        n1_l = load_list("n1_l", n1)
+        n2_l = load_list("n2_l", n2)
+        n3_l = load_list("n3_l", n3)
+        n5_l = load_list("n5_l", n5)
+        n4_l = load_list("n4_l", n4)
+        w_codes = keep.tile([P, 2 * N], U8, name="w_codes", align_bytes=64)
+        nc.sync.dma_start(w_codes[:].bitcast(I32), w1_words[0].bitcast(I32))
+        gain = keep.tile([P, PACK], F32, name="gain")
+        nc.gpsimd.dma_start(gain[:], gn.rearrange("(p t) o -> p (t o)", t=PACK))
+        w_plane = keep.tile([P, N], U8, name="w_plane", align_bytes=64)
+        nc.gpsimd.memset(w_plane[:].bitcast(I32), 0)
+        for q in range(4):
+            nc.gpsimd.dma_start(
+                w_plane[:].bitcast(I32)[32 * q : 32 * q + 4, :], w1_scales[0].bitcast(I32)[4 * q : 4 * q + 4, :]
+            )
+        neg_gain = keep.tile([P, PACK], F32, name="neg_gain")
+        nc.gpsimd.tensor_scalar(neg_gain[:], gain[:], -1.0, 0.0, ALU.mult, ALU.add)
+
+        d_bytes_got = keep.tile([P, 2 * H], U8, name="d_bytes_got")
+        x_bytes_got = keep.tile([P, S], U8, name="x_bytes_got")
+        nc.vector.tensor_copy(d_bytes_got[:, 0:H], d_bytes[:].indirect(ka_l[:]))
+        nc.vector.tensor_copy(d_bytes_got[:, H : 2 * H], d_bytes[:].indirect(kb_l[:]))
+        nc.vector.tensor_copy(x_bytes_got[:], x_bytes[:].indirect(offs_l[:]))
+        plane = keep.tile([P, 2 * H + S], U8, name="plane", align_bytes=64)
+        nc.vector.tensor_copy(
+            plane[:, 0 : 2 * H].rearrange("p (a t m) -> p a m t", a=2, t=PACK),
+            d_bytes_got[:].rearrange("p (a m t) -> p a m t", a=2, t=PACK),
+        )
+        nc.vector.tensor_copy(plane[:, 2 * H :].bitcast(I32), x_bytes_got[:].bitcast(I32))
+        plane_words = plane[:].bitcast(I32)
+        for e in range(1, 4):
+            nc.sync.dma_start(plane_words[e:P:32, :], plane_words[8 * e : P : 32, :])
+
+        x_got = keep.tile([P, S], U32, name="x_got", align_bytes=64)
+        nc.vector.tensor_copy(x_got[:], x_tab[:].indirect(offs_l[:]))
+        dealt = []
+        for name, lst in (("a", ka_l), ("b", kb_l)):
+            got = keep.tile([P, H], U32, name="got_" + name)
+            nc.vector.tensor_copy(got[:], d_tab[:].indirect(lst[:]))
+            codes = keep.tile([P, H], U32, name="codes_" + name, align_bytes=64)
+            nc.vector.tensor_copy(
+                codes[:].bitcast(I32).rearrange("p (t m) -> p m t", t=PACK),
+                got[:].bitcast(I32).rearrange("p (m t) -> p m t", t=PACK),
+            )
+            dealt.append(codes)
+
+        h = []
+        for t in range(PACK):
+            acc = psum.tile([P, S], F32, name="h_acc%d" % t)
+            for a in range(2):
+                nc.tensor.matmul_mx(
+                    out=acc[:],
+                    lhsT=dealt[a][:, P * t : P * (t + 1)].bitcast(FP8X4),
+                    lhsT_scale=plane[:, H * a + P * t : H * a + P * (t + 1)],
+                    rhs=x_got[:].bitcast(FP8X4),
+                    rhs_scale=plane[:, 2 * H :],
+                    start=(a == 0),
+                    stop=(a == 1),
+                )
+            h_t = keep.tile([P, S], F32, name="h%d" % t)
+            nc.vector.tensor_scalar(h_t[:], acc[:], 0.0625, None, ALU.mult)
+            h.append(h_t)
+
+        pa = [keep.tile([P, W], F32, name="pa%d" % t) for t in range(PACK)]
+        pb = [keep.tile([P, W], F32, name="pb%d" % t) for t in range(PACK)]
+        ra = [keep.tile([P, W], F32, name="ra%d" % t) for t in range(PACK)]
+        rb = [keep.tile([P, W], F32, name="rb%d" % t) for t in range(PACK)]
+        dt = [keep.tile([P, S], F32, name="dt%d" % t) for t in range(PACK)]
+        dt_gain = [keep.tile([P, S], F32, name="dt_gain%d" % t) for t in range(PACK)]
+        z_rows = [keep.tile([P, PACK, HALF], BF16, name="z_rows%d" % c) for c in range(2)]
+
+        def fetch_a(t):
+            nc.scalar.activation(pa[t][:], h[t][:].indirect(n1_l[:]), COPY)
+
+        def fetch_b(t):
+            nc.scalar.activation(pb[t][:], h[t][:].indirect(n2_l[:]), COPY)
+            nc.vector.tensor_tensor(ra[t][:], pa[t][:], pb[t][:], ALU.max)
+            nc.vector.tensor_tensor(rb[t][:], pa[t][:], pb[t][:], ALU.min)
+
+        def put_a(t):
+            nc.scalar.activation(dt[t][:].indirect(n1_l[:]), ra[t][:], COPY)
+
+        def put_b(t):
+            nc.scalar.activation(dt[t][:].indirect(n2_l[:]), rb[t][:], COPY)
+            nc.vector.tensor_scalar(dt_gain[t][:], dt[t][:], gain[:, t : t + 1], None, ALU.mult)
+
+        def differ(t, c):
+            cols = slice(HALF * c, HALF * (c + 1))
+            other = keep.tile([P, HALF], F32, name="other%d_%d" % (t, c))
+            nc.scalar.activation(other[:], dt[t][:].indirect(n3_l[:, 8 * c : 8 * (c + 1)]), COPY)
+            nc.vector.scalar_tensor_tensor(
+                z_rows[c][:, t, :], other[:], neg_gain[:, t : t + 1], dt_gain[t][:, cols], ALU.mult, ALU.add
+            )
+
+        h2_acc = [psum.tile([P, S], F32, name="h2_acc%d" % m) for m in range(N // P)]
+        h2 = [keep.tile([P, S], F32, name="h2_%d" % m) for m in range(N // P)]
+
+        def second_product(c):
+            cols = slice(HALF * c, HALF * (c + 1))
+            z_cols = keep.tile([P, HALF, PACK], BF16, name="z_cols%d" % c, align_bytes=64)
+            nc.vector.tensor_copy(z_cols[:], z_rows[c][:].rearrange("p t j -> p j t"))
+            z_codes = keep.tile([P, HALF], U32, name="z_codes%d" % c, align_bytes=64)
+            z_plane = keep.tile([P, HALF], U8, name="z_plane%d" % c, align_bytes=64)
+            nc.vector.quantize_mx(
+                out=z_codes[:].bitcast(FP8X4), scales=z_plane[:], in_=z_cols[:].rearrange("p j t -> p (j t)")
+            )
+            for m in range(N // P):
+                nc.tensor.matmul_mx(
+                    out=h2_acc[m][:, cols],
+                    lhsT=w_codes[:, 2 * P * m : 2 * P * (m + 1)].bitcast(FP4X4),
+                    lhsT_scale=w_plane[:, P * m : P * (m + 1)],
+                    rhs=z_codes[:].bitcast(FP8X4),
+                    rhs_scale=z_plane[:],
+                    start=True,
+                    stop=True,
+                )
+                nc.vector.tensor_copy(h2[m][:, cols], h2_acc[m][:, cols])
+
+        fetch_a(0)
+        fetch_b(0)
+        fetch_a(1)
+        fetch_b(1)
+        put_a(0)
+        fetch_a(2)
+        put_b(0)
+        fetch_b(2)
+        put_a(1)
+        fetch_a(3)
+        put_b(1)
+        fetch_b(3)
+        put_a(2)
+        differ(0, 0)
+        put_b(2)
+        differ(1, 0)
+        put_a(3)
+        differ(2, 0)
+        put_b(3)
+        differ(0, 1)
+        differ(3, 0)
+        second_product(0)
+        differ(1, 1)
+        differ(2, 1)
+        differ(3, 1)
+        second_product(1)
+
+        page_tags = ["page0", "page1", "x_then_page", "d_then_page"]
+        page = [keep.tile([P, U], F32, name="page%d" % m, tag=page_tags[m]) for m in range(N // P)]
+        larger = [keep.tile([P, S], F32, name="larger%d" % m) for m in range(N // P)]
+        for m in range(N // P):
+            nc.vector.memset(page[m][:], 0.0)
+
+        def fetch_rival(m):
+            rival = keep.tile([P, S], F32, name="rival%d" % m)
+            for c in range(2):
+                nc.scalar.activation(
+                    rival[:, HALF * c : HALF * (c + 1)], h2[m][:].indirect(n5_l[:, 8 * c : 8 * (c + 1)]), COPY
+                )
+            nc.vector.tensor_tensor(larger[m][:], h2[m][:], rival[:], ALU.max)
+
+        def put_page(m):
+            nc.scalar.activation(page[m][:].indirect(n4_l[:]), larger[m][:], COPY)
+            nc.sync.dma_start(out[P * m : P * (m + 1), :], page[m][:])
+
+        fetch_rival(0)
+        for m in range(N // P):
+            if m + 1 < N // P:
+                fetch_rival(m + 1)
+            put_page(m)

@@ -1,6 +1,7 @@
 from contextlib import ExitStack
 
 import concourse.mybir as mybir
+from concourse.masks import make_identity
 
 K, T, S, N, G, H, W, U = 512, 1024, 256, 512, 2048, 512, 128, 1024
 FLOPS = 2 * (2 * K * H * S + H * N * S)
@@ -19,6 +20,8 @@ COPY = mybir.ActivationFunctionType.Copy
 P = 128
 PACK = 4
 HALF = S // 2
+PIECE = H // 2
+TILES = H // P
 
 
 def tile_picked_haqorddpags_none_p_kernel(
@@ -34,94 +37,114 @@ def tile_picked_haqorddpags_none_p_kernel(
             nc.sync.dma_start(tile[:], src)
             return tile
 
-        x_bytes = keep.tile([P, T], U8, name="x_bytes")
-        d_bytes = keep.tile([P, G], U8, name="d_bytes")
-        for tile, rows in ((d_bytes, d_scales), (x_bytes, x_scales)):
+        def load_scale_rows(tile, rows):
             words = rows[0].bitcast(I32)
             nc.sync.dma_start(tile[:].bitcast(I32), words.unsqueeze(1).broadcast_to([16, 8, words.shape[1]]))
 
+        d_bytes = keep.tile([P, G], U8, name="d_bytes", tag="d_bytes_then_w_codes", align_bytes=64)
+        x_bytes = keep.tile([P, T], U8, name="x_bytes")
+        load_scale_rows(x_bytes, x_scales)
+        offs_l = load_list("offs_l", offs)
+        load_scale_rows(d_bytes, d_scales)
         ka_l = load_list("ka_l", ka)
         kb_l = load_list("kb_l", kb)
-        offs_l = load_list("offs_l", offs)
-        d_tab = keep.tile([P, G], U32, name="d_tab", tag="d_then_page")
-        x_tab = keep.tile([P, T], U32, name="x_tab", tag="x_then_page")
-        nc.sync.dma_start(d_tab[:].bitcast(I32), d_words[0].rearrange("p n t -> p (n t)").bitcast(I32))
-        nc.sync.dma_start(x_tab[:].bitcast(I32), x_words[0].rearrange("p n t -> p (n t)").bitcast(I32))
         n1_l = load_list("n1_l", n1)
         n2_l = load_list("n2_l", n2)
+        d_tab = keep.tile([P, G], U32, name="d_tab")
+        x_tab = keep.tile([P, T], U32, name="x_tab", tag="x_then_second", align_bytes=64)
+        nc.sync.dma_start(d_tab[:].bitcast(I32), d_words[0].rearrange("p n t -> p (n t)").bitcast(I32))
+        nc.sync.dma_start(x_tab[:].bitcast(I32), x_words[0].rearrange("p n t -> p (n t)").bitcast(I32))
         n3_l = load_list("n3_l", n3)
         n5_l = load_list("n5_l", n5)
         n4_l = load_list("n4_l", n4)
-        w_codes = keep.tile([P, 2 * N], U8, name="w_codes", align_bytes=64)
-        nc.sync.dma_start(w_codes[:].bitcast(I32), w1_words[0].bitcast(I32))
-        gain = keep.tile([P, PACK], F32, name="gain")
-        nc.gpsimd.dma_start(gain[:], gn.rearrange("(p t) o -> p (t o)", t=PACK))
-        w_plane = keep.tile([P, N], U8, name="w_plane", align_bytes=64)
-        nc.gpsimd.memset(w_plane[:].bitcast(I32), 0)
-        for q in range(4):
-            nc.gpsimd.dma_start(
-                w_plane[:].bitcast(I32)[32 * q : 32 * q + 4, :], w1_scales[0].bitcast(I32)[4 * q : 4 * q + 4, :]
-            )
-        neg_gain = keep.tile([P, PACK], F32, name="neg_gain")
-        nc.gpsimd.tensor_scalar(neg_gain[:], gain[:], -1.0, 0.0, ALU.mult, ALU.add)
+        gain = keep.tile([P, TILES], F32, name="gain")
+        with nc.allow_non_contiguous_dma(reason="one gain a partition and tile"):
+            nc.gpsimd.dma_start(gain[:], gn.rearrange("(t p) o -> p (t o)", p=P))
+        identity = keep.tile([P, P], F32, name="identity")
+        make_identity(nc, identity[:])
 
-        d_bytes_got = keep.tile([P, 2 * H], U8, name="d_bytes_got")
-        x_bytes_got = keep.tile([P, S], U8, name="x_bytes_got")
-        nc.vector.tensor_copy(d_bytes_got[:, 0:H], d_bytes[:].indirect(ka_l[:]))
-        nc.vector.tensor_copy(d_bytes_got[:, H : 2 * H], d_bytes[:].indirect(kb_l[:]))
-        nc.vector.tensor_copy(x_bytes_got[:], x_bytes[:].indirect(offs_l[:]))
-        plane = keep.tile([P, 2 * H + S], U8, name="plane", align_bytes=64)
-        nc.vector.tensor_copy(
-            plane[:, 0 : 2 * H].rearrange("p (a t m) -> p a m t", a=2, t=PACK),
-            d_bytes_got[:].rearrange("p (a m t) -> p a m t", a=2, t=PACK),
-        )
-        nc.vector.tensor_copy(plane[:, 2 * H :].bitcast(I32), x_bytes_got[:].bitcast(I32))
-        plane_words = plane[:].bitcast(I32)
-        for e in range(1, 4):
-            nc.sync.dma_start(plane_words[e:P:32, :], plane_words[8 * e : P : 32, :])
+        widths = (2 * PIECE + S, 2 * PIECE)
+        bytes_got = [keep.tile([P, widths[i]], U8, name="bytes_got%d" % i, tag="got%d" % i, align_bytes=64) for i in range(2)]
+        plane = [keep.tile([P, widths[i]], U8, name="plane%d" % i, align_bytes=64) for i in range(2)]
+        for i in range(2):
+            nc.vector.memset(plane[i][:].bitcast(I32), 0)
+
+        page = [keep.tile([P, U], F32, name="page%d" % m) for m in range(N // P)]
+        nc.vector.memset(page[0][:], 0.0)
+        for m in range(1, N // P):
+            nc.scalar.copy(page[m][:], page[0][:])
+
+        def piece_of(lst, i):
+            return lst[:, 16 * i : 16 * (i + 1)]
+
+        def gather_bytes(i):
+            if i == 0:
+                nc.vector.tensor_copy(bytes_got[i][:, 2 * PIECE :], x_bytes[:].indirect(offs_l[:]))
+            nc.vector.tensor_copy(bytes_got[i][:, 0:PIECE], d_bytes[:].indirect(piece_of(ka_l, i)))
+            nc.vector.tensor_copy(bytes_got[i][:, PIECE : 2 * PIECE], d_bytes[:].indirect(piece_of(kb_l, i)))
+            for e in range(4):
+                nc.sync.dma_start(plane[i][:].bitcast(I32)[e:P:32, :], bytes_got[i][:].bitcast(I32)[8 * e : P : 32, :])
 
         x_got = keep.tile([P, S], U32, name="x_got", align_bytes=64)
-        nc.vector.tensor_copy(x_got[:], x_tab[:].indirect(offs_l[:]))
-        dealt = []
-        for name, lst in (("a", ka_l), ("b", kb_l)):
-            got = keep.tile([P, H], U32, name="got_" + name)
-            nc.vector.tensor_copy(got[:], d_tab[:].indirect(lst[:]))
-            codes = keep.tile([P, H], U32, name="codes_" + name, align_bytes=64)
-            nc.vector.tensor_copy(
-                codes[:].bitcast(I32).rearrange("p (t m) -> p m t", t=PACK),
-                got[:].bitcast(I32).rearrange("p (m t) -> p m t", t=PACK),
-            )
-            dealt.append(codes)
+        first_got = [keep.tile([P, PIECE], U32, name="first_got%d" % a, align_bytes=64) for a in range(2)]
+        second_got = keep.tile([P, 2 * PIECE], U32, name="second_got", tag="x_then_second", align_bytes=64)
+        d_got = [[first_got[0][:], first_got[1][:]], [second_got[:, 0:PIECE], second_got[:, PIECE:]]]
 
-        h = []
-        for t in range(PACK):
-            acc = psum.tile([P, S], F32, name="h_acc%d" % t)
+        def gather_words(i):
+            nc.vector.tensor_copy(d_got[i][0], d_tab[:].indirect(piece_of(ka_l, i)))
+            nc.vector.tensor_copy(d_got[i][1], d_tab[:].indirect(piece_of(kb_l, i)))
+            if i == 0:
+                nc.vector.tensor_copy(x_got[:], x_tab[:].indirect(offs_l[:]))
+
+        h = [keep.tile([P, S], F32, name="h%d" % t) for t in range(TILES)]
+
+        def first_product(t):
+            i, off = divmod(P * t, PIECE)
+            acc = psum.tile([P, S], F32, name="h_acc%d" % t, tag="acc%d" % t)
             for a in range(2):
                 nc.tensor.matmul_mx(
                     out=acc[:],
-                    lhsT=dealt[a][:, P * t : P * (t + 1)].bitcast(FP8X4),
-                    lhsT_scale=plane[:, H * a + P * t : H * a + P * (t + 1)],
+                    lhsT=d_got[i][a][:, off : off + P].bitcast(FP8X4),
+                    lhsT_scale=plane[i][:, PIECE * a + off : PIECE * a + off + P],
                     rhs=x_got[:].bitcast(FP8X4),
-                    rhs_scale=plane[:, 2 * H :],
+                    rhs_scale=plane[0][:, 2 * PIECE :],
                     start=(a == 0),
                     stop=(a == 1),
                 )
-            h_t = keep.tile([P, S], F32, name="h%d" % t)
-            nc.vector.tensor_scalar(h_t[:], acc[:], 0.0625, None, ALU.mult)
-            h.append(h_t)
+            if t == 0:
+                nc.scalar.activation(h[t][:], acc[:], COPY, scale=0.0625)
+            else:
+                nc.vector.tensor_scalar(h[t][:], acc[:], 0.0625, None, ALU.mult)
 
-        pa = [keep.tile([P, W], F32, name="pa%d" % t) for t in range(PACK)]
-        pb = [keep.tile([P, W], F32, name="pb%d" % t) for t in range(PACK)]
-        ra = [keep.tile([P, W], F32, name="ra%d" % t) for t in range(PACK)]
-        rb = [keep.tile([P, W], F32, name="rb%d" % t) for t in range(PACK)]
-        dt = [keep.tile([P, S], F32, name="dt%d" % t) for t in range(PACK)]
-        dt_gain = [keep.tile([P, S], F32, name="dt_gain%d" % t) for t in range(PACK)]
-        z_rows = [keep.tile([P, PACK, HALF], BF16, name="z_rows%d" % c) for c in range(2)]
+        gather_bytes(0)
+        gather_bytes(1)
+        gather_words(0)
+        first_product(0)
+        first_product(1)
+        gather_words(1)
+        first_product(2)
+        first_product(3)
 
-        def fetch_a(t):
+        w_codes = keep.tile([P, 2 * N], U8, name="w_codes", tag="d_bytes_then_w_codes", align_bytes=64)
+        nc.sync.dma_start(w_codes[:].bitcast(I32), w1_words[0].bitcast(I32))
+        w_plane = keep.tile([P, N], U8, name="w_plane", tag="got1", align_bytes=64)
+        nc.vector.memset(w_plane[:].bitcast(I32), 0)
+        for q in range(4):
+            nc.sync.dma_start(
+                w_plane[:].bitcast(I32)[32 * q : 32 * q + 4, :], w1_scales[0].bitcast(I32)[4 * q : 4 * q + 4, :]
+            )
+
+        pa = [keep.tile([P, W], F32, name="pa%d" % t) for t in range(TILES)]
+        pb = [keep.tile([P, W], F32, name="pb%d" % t) for t in range(TILES)]
+        ra = [keep.tile([P, W], F32, name="ra%d" % t) for t in range(TILES)]
+        rb = [keep.tile([P, W], F32, name="rb%d" % t, tag="rb%d" % t) for t in range(TILES)]
+        dt = [keep.tile([P, S], F32, name="dt%d" % t) for t in range(TILES)]
+        dt_gain = [keep.tile([P, S], F32, name="dt_gain%d" % t) for t in range(TILES)]
+        turn_acc = [psum.tile([P, H], F32, name="turn_acc%d" % c, tag="turn%d" % c) for c in range(2)]
+        z_turned = [keep.tile([P, H], BF16, name="z_turned%d" % c) for c in range(2)]
+
+        def fetch_pair(t):
             nc.scalar.activation(pa[t][:], h[t][:].indirect(n1_l[:]), COPY)
-
-        def fetch_b(t):
             nc.scalar.activation(pb[t][:], h[t][:].indirect(n2_l[:]), COPY)
             nc.vector.tensor_tensor(ra[t][:], pa[t][:], pb[t][:], ALU.max)
             nc.vector.tensor_tensor(rb[t][:], pa[t][:], pb[t][:], ALU.min)
@@ -133,78 +156,81 @@ def tile_picked_haqorddpags_none_p_kernel(
             nc.scalar.activation(dt[t][:].indirect(n2_l[:]), rb[t][:], COPY)
             nc.vector.tensor_scalar(dt_gain[t][:], dt[t][:], gain[:, t : t + 1], None, ALU.mult)
 
-        def differ(t, c):
+        def differ(t, c, minus, acc):
             cols = slice(HALF * c, HALF * (c + 1))
-            other = keep.tile([P, HALF], F32, name="other%d_%d" % (t, c))
-            nc.scalar.activation(other[:], dt[t][:].indirect(n3_l[:, 8 * c : 8 * (c + 1)]), COPY)
-            nc.vector.scalar_tensor_tensor(
-                z_rows[c][:, t, :], other[:], neg_gain[:, t : t + 1], dt_gain[t][:, cols], ALU.mult, ALU.add
+            nc.scalar.activation(minus, dt_gain[t][:].indirect(n3_l[:, 8 * c : 8 * (c + 1)]), COPY, scale=-1.0)
+            nc.tensor.matmul(acc, dt_gain[t][:, cols], identity[:], start=True, stop=False, is_transpose=True)
+            nc.tensor.matmul(acc, minus, identity[:], start=False, stop=True, is_transpose=True)
+
+        h2 = [keep.tile([P, S + 8], F32, name="h2_%d" % m) for m in range(N // P)]
+        z_cols = [keep.tile([P, HALF * PACK], BF16, name="z_cols%d" % c, align_bytes=64) for c in range(2)]
+        z_codes = [keep.tile([P, HALF], U32, name="z_codes%d" % c, align_bytes=64) for c in range(2)]
+        z_plane = [keep.tile([P, HALF], U8, name="z_plane%d" % c, align_bytes=64) for c in range(2)]
+
+        def turn_back(c, copy):
+            pairs = z_turned[c][:].bitcast(F32)
+            back = psum.tile([P, 2, HALF], F32, name="back%d" % c, tag="back%d" % c)
+            for u in range(2):
+                nc.tensor.transpose(back[:, u, :], pairs[:, u : H // 2 : 2], identity[:])
+            copy(z_cols[c][:].bitcast(F32).rearrange("p (j u) -> p j u", u=2), back[:].rearrange("p u j -> p j u"))
+            nc.vector.quantize_mx(out=z_codes[c][:].bitcast(FP8X4), scales=z_plane[c][:], in_=z_cols[c][:])
+
+        def second_product(m, c, acc):
+            nc.tensor.matmul_mx(
+                out=acc,
+                lhsT=w_codes[:, 2 * P * m : 2 * P * (m + 1)].bitcast(FP4X4),
+                lhsT_scale=w_plane[:, P * m : P * (m + 1)],
+                rhs=z_codes[c][:].bitcast(FP8X4),
+                rhs_scale=z_plane[c][:],
+                start=True,
+                stop=True,
             )
 
-        h2_acc = [psum.tile([P, S], F32, name="h2_acc%d" % m) for m in range(N // P)]
-        h2 = [keep.tile([P, S], F32, name="h2_%d" % m) for m in range(N // P)]
+        def differ_and_round(t, c):
+            rows = slice(P * t, P * (t + 1))
+            minus = keep.tile([P, HALF], F32, name="minus%d_%d" % (t, c))
+            differ(t, c, minus[:], turn_acc[c][:, rows])
+            nc.vector.tensor_copy(z_turned[c][:, rows], turn_acc[c][:, rows])
 
-        def second_product(c):
-            cols = slice(HALF * c, HALF * (c + 1))
-            z_cols = keep.tile([P, HALF, PACK], BF16, name="z_cols%d" % c, align_bytes=64)
-            nc.vector.tensor_copy(z_cols[:], z_rows[c][:].rearrange("p t j -> p j t"))
-            z_codes = keep.tile([P, HALF], U32, name="z_codes%d" % c, align_bytes=64)
-            z_plane = keep.tile([P, HALF], U8, name="z_plane%d" % c, align_bytes=64)
-            nc.vector.quantize_mx(
-                out=z_codes[:].bitcast(FP8X4), scales=z_plane[:], in_=z_cols[:].rearrange("p j t -> p (j t)")
-            )
-            for m in range(N // P):
-                nc.tensor.matmul_mx(
-                    out=h2_acc[m][:, cols],
-                    lhsT=w_codes[:, 2 * P * m : 2 * P * (m + 1)].bitcast(FP4X4),
-                    lhsT_scale=w_plane[:, P * m : P * (m + 1)],
-                    rhs=z_codes[:].bitcast(FP8X4),
-                    rhs_scale=z_plane[:],
-                    start=True,
-                    stop=True,
-                )
-                nc.vector.tensor_copy(h2[m][:, cols], h2_acc[m][:, cols])
-
-        fetch_a(0)
-        fetch_b(0)
-        fetch_a(1)
-        fetch_b(1)
+        fetch_pair(0)
+        fetch_pair(1)
         put_a(0)
-        fetch_a(2)
-        put_b(0)
-        fetch_b(2)
         put_a(1)
-        fetch_a(3)
+        put_b(0)
         put_b(1)
-        fetch_b(3)
+        fetch_pair(2)
+        fetch_pair(3)
+        differ_and_round(0, 0)
+        differ_and_round(0, 1)
         put_a(2)
-        differ(0, 0)
-        put_b(2)
-        differ(1, 0)
         put_a(3)
-        differ(2, 0)
+        put_b(2)
+        differ_and_round(1, 0)
+        differ_and_round(1, 1)
         put_b(3)
-        differ(0, 1)
-        differ(3, 0)
-        second_product(0)
-        differ(1, 1)
-        differ(2, 1)
-        differ(3, 1)
-        second_product(1)
+        differ_and_round(2, 0)
+        differ_and_round(2, 1)
+        differ_and_round(3, 0)
+        differ_and_round(3, 1)
+        turn_back(0, nc.scalar.copy)
+        turn_back(1, nc.vector.tensor_copy)
+        h2_acc = [psum.tile([P, S], F32, name="h2_acc%d" % m, tag="acc%d" % m) for m in range(N // P)]
+        corner = psum.tile([P, HALF], F32, name="corner", tag="turn0")
+        second_product(0, 0, corner[:])
+        nc.scalar.copy(h2[0][:, 0:HALF], corner[:])
+        second_product(0, 1, h2_acc[0][:, HALF:])
+        nc.scalar.copy(h2[0][:, HALF:S], h2_acc[0][:, HALF:])
+        for m in range(1, N // P):
+            second_product(m, 0, h2_acc[m][:, 0:HALF])
+            second_product(m, 1, h2_acc[m][:, HALF:])
+            nc.vector.tensor_copy(h2[m][:, 0:S], h2_acc[m][:])
 
-        page_tags = ["page0", "page1", "x_then_page", "d_then_page"]
-        page = [keep.tile([P, U], F32, name="page%d" % m, tag=page_tags[m]) for m in range(N // P)]
         larger = [keep.tile([P, S], F32, name="larger%d" % m) for m in range(N // P)]
-        for m in range(N // P):
-            nc.vector.memset(page[m][:], 0.0)
 
         def fetch_rival(m):
             rival = keep.tile([P, S], F32, name="rival%d" % m)
-            for c in range(2):
-                nc.scalar.activation(
-                    rival[:, HALF * c : HALF * (c + 1)], h2[m][:].indirect(n5_l[:, 8 * c : 8 * (c + 1)]), COPY
-                )
-            nc.vector.tensor_tensor(larger[m][:], h2[m][:], rival[:], ALU.max)
+            nc.scalar.activation(rival[:], h2[m][:].indirect(n5_l[:]), COPY)
+            nc.vector.tensor_tensor(larger[m][:], h2[m][:, 0:S], rival[:], ALU.max)
 
         def put_page(m):
             nc.scalar.activation(page[m][:].indirect(n4_l[:]), larger[m][:], COPY)

@@ -57,9 +57,6 @@ def tile_picked_haqorddpags_none_p_kernel(
         n3_l = load_list("n3_l", n3)
         n5_l = load_list("n5_l", n5)
         n4_l = load_list("n4_l", n4)
-        gain = keep.tile([P, TILES], F32, name="gain")
-        with nc.allow_non_contiguous_dma(reason="one gain a partition and tile"):
-            nc.gpsimd.dma_start(gain[:], gn.rearrange("(t p) o -> p (t o)", p=P))
         identity = keep.tile([P, P], F32, name="identity")
         make_identity(nc, identity[:])
 
@@ -96,7 +93,7 @@ def tile_picked_haqorddpags_none_p_kernel(
             if i == 0:
                 nc.vector.tensor_copy(x_got[:], x_tab[:].indirect(offs_l[:]))
 
-        h = [keep.tile([P, S], F32, name="h%d" % t) for t in range(TILES)]
+        h = [keep.tile([P, S], F32, name="h%d" % t, tag="h%d" % t) for t in range(TILES)]
 
         def first_product(t):
             i, off = divmod(P * t, PIECE)
@@ -121,6 +118,9 @@ def tile_picked_haqorddpags_none_p_kernel(
         gather_words(0)
         first_product(0)
         first_product(1)
+        gain = keep.tile([P, TILES], F32, name="gain", tag="got0", align_bytes=64)
+        with nc.allow_non_contiguous_dma(reason="one gain a partition and tile"):
+            nc.sync.dma_start(gain[:], gn.rearrange("(t p) o -> p (t o)", p=P))
         gather_words(1)
         first_product(2)
         first_product(3)
@@ -137,23 +137,27 @@ def tile_picked_haqorddpags_none_p_kernel(
         pa = [keep.tile([P, W], F32, name="pa%d" % t) for t in range(TILES)]
         pb = [keep.tile([P, W], F32, name="pb%d" % t) for t in range(TILES)]
         ra = [keep.tile([P, W], F32, name="ra%d" % t) for t in range(TILES)]
-        rb = [keep.tile([P, W], F32, name="rb%d" % t, tag="rb%d" % t) for t in range(TILES)]
+        rb = {}
         dt = [keep.tile([P, S], F32, name="dt%d" % t) for t in range(TILES)]
         dt_gain = [keep.tile([P, S], F32, name="dt_gain%d" % t) for t in range(TILES)]
-        turn_acc = [psum.tile([P, H], F32, name="turn_acc%d" % c, tag="turn%d" % c) for c in range(2)]
+        turn_banks = (("back0", "back1"), ("acc0", "acc1"), ("acc2", "acc3"), ("turn0", "turn1"))
         z_turned = [keep.tile([P, H], BF16, name="z_turned%d" % c) for c in range(2)]
 
-        def fetch_pair(t):
-            nc.scalar.activation(pa[t][:], h[t][:].indirect(n1_l[:]), COPY)
-            nc.scalar.activation(pb[t][:], h[t][:].indirect(n2_l[:]), COPY)
-            nc.vector.tensor_tensor(ra[t][:], pa[t][:], pb[t][:], ALU.max)
-            nc.vector.tensor_tensor(rb[t][:], pa[t][:], pb[t][:], ALU.min)
+        def fetch_pairs(first):
+            for t in (first, first + 1):
+                nc.scalar.activation(pa[t][:], h[t][:].indirect(n1_l[:]), COPY)
+                nc.scalar.activation(pb[t][:], h[t][:].indirect(n2_l[:]), COPY)
+                nc.vector.tensor_tensor(ra[t][:], pa[t][:], pb[t][:], ALU.max)
+            smaller = keep.tile([P, 2 * W], F32, name="smaller%d" % first, tag="h%d" % (first + 1))
+            for t in (first, first + 1):
+                rb[t] = smaller[:, W * (t - first) : W * (t - first + 1)]
+                nc.vector.tensor_tensor(rb[t], pa[t][:], pb[t][:], ALU.min)
 
         def put_a(t):
             nc.scalar.activation(dt[t][:].indirect(n1_l[:]), ra[t][:], COPY)
 
         def put_b(t):
-            nc.scalar.activation(dt[t][:].indirect(n2_l[:]), rb[t][:], COPY)
+            nc.scalar.activation(dt[t][:].indirect(n2_l[:]), rb[t], COPY)
             nc.vector.tensor_scalar(dt_gain[t][:], dt[t][:], gain[:, t : t + 1], None, ALU.mult)
 
         def differ(t, c, minus, acc):
@@ -187,19 +191,17 @@ def tile_picked_haqorddpags_none_p_kernel(
             )
 
         def differ_and_round(t, c):
-            rows = slice(P * t, P * (t + 1))
             minus = keep.tile([P, HALF], F32, name="minus%d_%d" % (t, c))
-            differ(t, c, minus[:], turn_acc[c][:, rows])
-            nc.vector.tensor_copy(z_turned[c][:, rows], turn_acc[c][:, rows])
+            turned = psum.tile([P, P], F32, name="turned%d_%d" % (t, c), tag=turn_banks[t][c])
+            differ(t, c, minus[:], turned[:])
+            nc.vector.tensor_copy(z_turned[c][:, P * t : P * (t + 1)], turned[:])
 
-        fetch_pair(0)
-        fetch_pair(1)
+        fetch_pairs(0)
         put_a(0)
         put_a(1)
         put_b(0)
         put_b(1)
-        fetch_pair(2)
-        fetch_pair(3)
+        fetch_pairs(2)
         differ_and_round(0, 0)
         differ_and_round(0, 1)
         put_a(2)

from contextlib import ExitStack

import concourse.mybir as mybir
from concourse.masks import make_identity

K, T, S, N, G, H, W, U = 512, 1024, 256, 512, 2048, 512, 128, 1024
FLOPS = 2 * (2 * K * H * S + H * N * S)

F32 = mybir.dt.float32
BF16 = mybir.dt.bfloat16
I32 = mybir.dt.int32
U32 = mybir.dt.uint32
U16 = mybir.dt.uint16
U8 = mybir.dt.uint8
FP8X4 = mybir.dt.float8_e4m3fn_x4
FP4X4 = mybir.dt.float4_e2m1fn_x4
ALU = mybir.AluOpType
COPY = mybir.ActivationFunctionType.Copy

P = 128
PACK = 4
HALF = S // 2
PIECE = H // 2
TILES = H // P


def tile_picked_haqorddpags_none_p_kernel(
    tc, x_words, x_scales, d_words, d_scales, gn, w1_words, w1_scales, offs, ka, kb, n1, n2, n3, n4, n5, out
):
    nc = tc.nc
    with ExitStack() as ctx:
        keep = ctx.enter_context(tc.tile_pool(name="keep", bufs=1))
        psum = ctx.enter_context(tc.psum_pool(name="psum", bufs=1))

        def load_list(name, src):
            tile = keep.tile(list(src.shape), U16, name=name)
            nc.sync.dma_start(tile[:], src)
            return tile

        def load_scale_rows(tile, rows):
            words = rows[0].bitcast(I32)
            nc.sync.dma_start(tile[:].bitcast(I32), words.unsqueeze(1).broadcast_to([16, 8, words.shape[1]]))

        d_bytes = keep.tile([P, G], U8, name="d_bytes", tag="d_bytes_then_w_codes", align_bytes=64)
        x_bytes = keep.tile([P, T], U8, name="x_bytes")
        load_scale_rows(x_bytes, x_scales)
        offs_l = load_list("offs_l", offs)
        load_scale_rows(d_bytes, d_scales)
        ka_l = load_list("ka_l", ka)
        kb_l = load_list("kb_l", kb)
        n1_l = load_list("n1_l", n1)
        n2_l = load_list("n2_l", n2)
        d_tab = keep.tile([P, G], U32, name="d_tab")
        x_tab = keep.tile([P, T], U32, name="x_tab", tag="x_then_second", align_bytes=64)
        nc.sync.dma_start(d_tab[:].bitcast(I32), d_words[0].rearrange("p n t -> p (n t)").bitcast(I32))
        nc.sync.dma_start(x_tab[:].bitcast(I32), x_words[0].rearrange("p n t -> p (n t)").bitcast(I32))
        n3_l = load_list("n3_l", n3)
        n5_l = load_list("n5_l", n5)
        n4_l = load_list("n4_l", n4)
        identity = keep.tile([P, P], F32, name="identity")
        make_identity(nc, identity[:])

        widths = (2 * PIECE + S, 2 * PIECE)
        bytes_got = [keep.tile([P, widths[i]], U8, name="bytes_got%d" % i, tag="got%d" % i, align_bytes=64) for i in range(2)]
        plane = [keep.tile([P, widths[i]], U8, name="plane%d" % i, align_bytes=64) for i in range(2)]
        for i in range(2):
            nc.vector.memset(plane[i][:].bitcast(I32), 0)

        page = [keep.tile([P, U], F32, name="page%d" % m) for m in range(N // P)]
        nc.vector.memset(page[0][:], 0.0)
        for m in range(1, N // P):
            nc.scalar.copy(page[m][:], page[0][:])

        def piece_of(lst, i):
            return lst[:, 16 * i : 16 * (i + 1)]

        def gather_bytes(i):
            if i == 0:
                nc.vector.tensor_copy(bytes_got[i][:, 2 * PIECE :], x_bytes[:].indirect(offs_l[:]))
            nc.vector.tensor_copy(bytes_got[i][:, 0:PIECE], d_bytes[:].indirect(piece_of(ka_l, i)))
            nc.vector.tensor_copy(bytes_got[i][:, PIECE : 2 * PIECE], d_bytes[:].indirect(piece_of(kb_l, i)))
            for e in range(4):
                nc.sync.dma_start(plane[i][:].bitcast(I32)[e:P:32, :], bytes_got[i][:].bitcast(I32)[8 * e : P : 32, :])

        x_got = keep.tile([P, S], U32, name="x_got", align_bytes=64)
        first_got = [keep.tile([P, PIECE], U32, name="first_got%d" % a, align_bytes=64) for a in range(2)]
        second_got = keep.tile([P, 2 * PIECE], U32, name="second_got", tag="x_then_second", align_bytes=64)
        d_got = [[first_got[0][:], first_got[1][:]], [second_got[:, 0:PIECE], second_got[:, PIECE:]]]

        def gather_words(i):
            nc.vector.tensor_copy(d_got[i][0], d_tab[:].indirect(piece_of(ka_l, i)))
            nc.vector.tensor_copy(d_got[i][1], d_tab[:].indirect(piece_of(kb_l, i)))
            if i == 0:
                nc.vector.tensor_copy(x_got[:], x_tab[:].indirect(offs_l[:]))

        h = [keep.tile([P, S], F32, name="h%d" % t, tag="h%d" % t) for t in range(TILES)]

        def first_product(t):
            i, off = divmod(P * t, PIECE)
            acc = psum.tile([P, S], F32, name="h_acc%d" % t, tag="acc%d" % t)
            for a in range(2):
                nc.tensor.matmul_mx(
                    out=acc[:],
                    lhsT=d_got[i][a][:, off : off + P].bitcast(FP8X4),
                    lhsT_scale=plane[i][:, PIECE * a + off : PIECE * a + off + P],
                    rhs=x_got[:].bitcast(FP8X4),
                    rhs_scale=plane[0][:, 2 * PIECE :],
                    start=(a == 0),
                    stop=(a == 1),
                )
            if t == 0:
                nc.scalar.activation(h[t][:], acc[:], COPY, scale=0.0625)
            else:
                nc.vector.tensor_scalar(h[t][:], acc[:], 0.0625, None, ALU.mult)

        gather_bytes(0)
        gather_bytes(1)
        gather_words(0)
        first_product(0)
        first_product(1)
        gain = keep.tile([P, TILES], F32, name="gain", tag="got0", align_bytes=64)
        with nc.allow_non_contiguous_dma(reason="one gain a partition and tile"):
            nc.sync.dma_start(gain[:], gn.rearrange("(t p) o -> p (t o)", p=P))
        gather_words(1)
        first_product(2)
        first_product(3)

        w_codes = keep.tile([P, 2 * N], U8, name="w_codes", tag="d_bytes_then_w_codes", align_bytes=64)
        nc.sync.dma_start(w_codes[:].bitcast(I32), w1_words[0].bitcast(I32))
        w_plane = keep.tile([P, N], U8, name="w_plane", tag="got1", align_bytes=64)
        nc.vector.memset(w_plane[:].bitcast(I32), 0)
        for q in range(4):
            nc.sync.dma_start(
                w_plane[:].bitcast(I32)[32 * q : 32 * q + 4, :], w1_scales[0].bitcast(I32)[4 * q : 4 * q + 4, :]
            )

        pa = [keep.tile([P, W], F32, name="pa%d" % t) for t in range(TILES)]
        pb = [keep.tile([P, W], F32, name="pb%d" % t) for t in range(TILES)]
        ra = [keep.tile([P, W], F32, name="ra%d" % t) for t in range(TILES)]
        rb = {}
        dt = [keep.tile([P, S], F32, name="dt%d" % t) for t in range(TILES)]
        dt_gain = [keep.tile([P, S], F32, name="dt_gain%d" % t) for t in range(TILES)]
        turn_banks = (("back0", "back1"), ("acc0", "acc1"), ("acc2", "acc3"), ("turn0", "turn1"))
        z_turned = [keep.tile([P, H], BF16, name="z_turned%d" % c) for c in range(2)]

        def fetch_pairs(first):
            for t in (first, first + 1):
                nc.scalar.activation(pa[t][:], h[t][:].indirect(n1_l[:]), COPY)
                nc.scalar.activation(pb[t][:], h[t][:].indirect(n2_l[:]), COPY)
                nc.vector.tensor_tensor(ra[t][:], pa[t][:], pb[t][:], ALU.max)
            smaller = keep.tile([P, 2 * W], F32, name="smaller%d" % first, tag="h%d" % (first + 1))
            for t in (first, first + 1):
                rb[t] = smaller[:, W * (t - first) : W * (t - first + 1)]
                nc.vector.tensor_tensor(rb[t], pa[t][:], pb[t][:], ALU.min)

        def put_a(t):
            nc.scalar.activation(dt[t][:].indirect(n1_l[:]), ra[t][:], COPY)

        def put_b(t):
            nc.scalar.activation(dt[t][:].indirect(n2_l[:]), rb[t], COPY)
            nc.vector.tensor_scalar(dt_gain[t][:], dt[t][:], gain[:, t : t + 1], None, ALU.mult)

        def differ(t, c, minus, acc):
            cols = slice(HALF * c, HALF * (c + 1))
            nc.scalar.activation(minus, dt_gain[t][:].indirect(n3_l[:, 8 * c : 8 * (c + 1)]), COPY, scale=-1.0)
            nc.tensor.matmul(acc, dt_gain[t][:, cols], identity[:], start=True, stop=False, is_transpose=True)
            nc.tensor.matmul(acc, minus, identity[:], start=False, stop=True, is_transpose=True)

        h2 = [keep.tile([P, S + 8], F32, name="h2_%d" % m) for m in range(N // P)]
        z_cols = [keep.tile([P, HALF * PACK], BF16, name="z_cols%d" % c, align_bytes=64) for c in range(2)]
        z_codes = [keep.tile([P, HALF], U32, name="z_codes%d" % c, align_bytes=64) for c in range(2)]
        z_plane = [keep.tile([P, HALF], U8, name="z_plane%d" % c, align_bytes=64) for c in range(2)]

        def turn_back(c, copy):
            pairs = z_turned[c][:].bitcast(F32)
            back = psum.tile([P, 2, HALF], F32, name="back%d" % c, tag="back%d" % c)
            for u in range(2):
                nc.tensor.transpose(back[:, u, :], pairs[:, u : H // 2 : 2], identity[:])
            copy(z_cols[c][:].bitcast(F32).rearrange("p (j u) -> p j u", u=2), back[:].rearrange("p u j -> p j u"))
            nc.vector.quantize_mx(out=z_codes[c][:].bitcast(FP8X4), scales=z_plane[c][:], in_=z_cols[c][:])

        def second_product(m, c, acc):
            nc.tensor.matmul_mx(
                out=acc,
                lhsT=w_codes[:, 2 * P * m : 2 * P * (m + 1)].bitcast(FP4X4),
                lhsT_scale=w_plane[:, P * m : P * (m + 1)],
                rhs=z_codes[c][:].bitcast(FP8X4),
                rhs_scale=z_plane[c][:],
                start=True,
                stop=True,
            )

        def differ_and_round(t, c):
            minus = keep.tile([P, HALF], F32, name="minus%d_%d" % (t, c))
            turned = psum.tile([P, P], F32, name="turned%d_%d" % (t, c), tag=turn_banks[t][c])
            differ(t, c, minus[:], turned[:])
            nc.vector.tensor_copy(z_turned[c][:, P * t : P * (t + 1)], turned[:])

        fetch_pairs(0)
        put_a(0)
        put_a(1)
        put_b(0)
        put_b(1)
        fetch_pairs(2)
        differ_and_round(0, 0)
        differ_and_round(0, 1)
        put_a(2)
        put_a(3)
        put_b(2)
        differ_and_round(1, 0)
        differ_and_round(1, 1)
        put_b(3)
        differ_and_round(2, 0)
        differ_and_round(2, 1)
        differ_and_round(3, 0)
        differ_and_round(3, 1)
        turn_back(0, nc.scalar.copy)
        turn_back(1, nc.vector.tensor_copy)
        h2_acc = [psum.tile([P, S], F32, name="h2_acc%d" % m, tag="acc%d" % m) for m in range(N // P)]
        corner = psum.tile([P, HALF], F32, name="corner", tag="turn0")
        second_product(0, 0, corner[:])
        nc.scalar.copy(h2[0][:, 0:HALF], corner[:])
        second_product(0, 1, h2_acc[0][:, HALF:])
        nc.scalar.copy(h2[0][:, HALF:S], h2_acc[0][:, HALF:])
        for m in range(1, N // P):
            second_product(m, 0, h2_acc[m][:, 0:HALF])
            second_product(m, 1, h2_acc[m][:, HALF:])
            nc.vector.tensor_copy(h2[m][:, 0:S], h2_acc[m][:])

        larger = [keep.tile([P, S], F32, name="larger%d" % m) for m in range(N // P)]

        def fetch_rival(m):
            rival = keep.tile([P, S], F32, name="rival%d" % m)
            nc.scalar.activation(rival[:], h2[m][:].indirect(n5_l[:]), COPY)
            nc.vector.tensor_tensor(larger[m][:], h2[m][:, 0:S], rival[:], ALU.max)

        def put_page(m):
            nc.scalar.activation(page[m][:].indirect(n4_l[:]), larger[m][:], COPY)
            nc.sync.dma_start(out[P * m : P * (m + 1), :], page[m][:])

        fetch_rival(0)
        for m in range(N // P):
            if m + 1 < N // P:
                fetch_rival(m + 1)
            put_page(m)
